import numpy as np
import ml_dtypes


def mxq(x, axis, fmt="e4m3"):
    dtype, down = {"e4m3": (ml_dtypes.float8_e4m3fn, 7), "e5m2": (ml_dtypes.float8_e5m2, 14)}[fmt]
    v = np.moveaxis(np.asarray(x, np.float32).astype(ml_dtypes.bfloat16).astype(np.float64), axis, -1)
    blocks = v.reshape(v.shape[:-1] + (-1, 32))
    amax = np.abs(blocks).max(-1, keepdims=True)
    byte = np.maximum(np.where(amax > 0, np.frexp(amax)[1] - 1 + 127, 0) - down, 1)
    scale = np.exp2(byte - 127.0)
    codes = (blocks / scale).astype(np.float32).astype(dtype).astype(np.float64)
    return np.moveaxis((codes * scale).reshape(v.shape), -1, axis)


WIDE = False


def mx_kscale(k, group=512):
    if not WIDE:
        return np.ones(k)
    levels = np.array([10, -10, 5, -5, 0])
    if group != 512:
        return np.exp2(np.random.permutation(np.resize(levels, k // group))).repeat(group)
    if k % 512:
        return np.exp2(np.random.permutation(np.resize(levels, k // 32))).repeat(32)
    a = np.empty((k // 512, 16))
    for p in range(k // 512):
        a[p, :8] = np.random.permutation(np.resize(levels, 8))
        for g in range(8):
            far = levels[np.abs(levels - a[p, g]) >= 10]
            a[p, g + 8] = far[np.random.randint(len(far))]
    return np.exp2(a.ravel()).repeat(32)


def f64(x):
    return np.asarray(x).astype(np.float64)


def bf(x):
    return np.asarray(x, np.float32).astype(ml_dtypes.bfloat16)


def planes(Y):
    r, m = Y.shape
    b = f64(bf(Y)).reshape(r // 32, 32, m)
    amax = np.abs(b).max(1)
    byte = np.clip(np.where(amax > 0, np.frexp(amax)[1] - 1 + 127 - 7, 1), 1, 254)
    codes = (b * np.exp2(127.0 - byte)[:, None, :]).reshape(r, m).astype(np.float32).astype(ml_dtypes.float8_e4m3fn).view(np.uint8)
    words = codes.reshape(r // 512, 128, 4, m).transpose(0, 1, 3, 2)
    return np.ascontiguousarray(words), np.ascontiguousarray(byte.astype(np.uint8).reshape(r // 512, 16, m))


G, D, M, N = 2, 256, 256, 512


def setup_inputs():
    n = np.random.standard_normal
    s_d = mx_kscale(D, 0)
    return {
        "x": (n((G, D, N)) * s_d[:, None]).astype(np.float32),
        "w1": (n((G, D, M)) / np.sqrt(D) / s_d[:, None]).astype(np.float32),
        "w2": (n((G, D, M)) / np.sqrt(D) / s_d[:, None]).astype(np.float32),
        "tp": (np.random.uniform(0.6, 2.0, (G, M, 1))).astype(np.float32),
        "dx": (n((G, D, N)) * s_d[:, None]).astype(np.float32),
        "og": (np.random.uniform(0.5, 2.0, (G, M, 1))).astype(np.float32),
        "base": (0.3 * n((G, M, N))).astype(np.float32),
    }


def reference(x, w1, w2, tp, dx, og, base):
    w1q = mxq(f64(w1), 1, "e4m3")
    xq = mxq(f64(x), 1, "e4m3")
    z1 = w1q.transpose(0, 2, 1) @ xq
    dxq = mxq(f64(dx), 1, "e4m3")
    tz1 = w1q.transpose(0, 2, 1) @ dxq
    w2q = mxq(f64(w2), 1, "e4m3")
    z2 = w2q.transpose(0, 2, 1) @ xq
    tz2 = w2q.transpose(0, 2, 1) @ dxq
    se = np.exp(z1 * f64(tp)) + np.exp(z2 * f64(tp))
    xse = tz1 * f64(tp) * np.exp(z1 * f64(tp)) + tz2 * f64(tp) * np.exp(z2 * f64(tp))
    xh = xse / se / f64(tp)
    y = xh * f64(og) + f64(base)
    Y = y.reshape(G * M, N)
    words, scales = planes(Y)
    return Y, words, scales

@@ -1,0 +1,248 @@
+from contextlib import ExitStack
+
+import concourse.mybir as mybir
+
+G, D, M, N = 2, 256, 256, 512
+FLOPS = 4 * 2 * G * D * M * N
+
+F32 = mybir.dt.float32
+BF16 = mybir.dt.bfloat16
+U32 = mybir.dt.uint32
+I32 = mybir.dt.int32
+U8 = mybir.dt.uint8
+FP8X4 = mybir.dt.float8_e4m3fn_x4
+ACT = mybir.ActivationFunctionType
+ALU = mybir.AluOpType
+
+P = 128
+PACK = 4
+ROWS = D // PACK
+HALVES = M // P
+CHUNK = 256
+CHUNKS = N // CHUNK
+MM_N = 128
+VEC_COLS = 176
+
+
+def tile_rows_pl_tnsoftmaxoftwo_kernel(tc, x, w1, w2, tp, dx, og, base, out_0, out_1, out_2):
+    nc = tc.nc
+    with ExitStack() as ctx:
+        sb = ctx.enter_context(tc.tile_pool(name="sb", bufs=1))
+        ps = ctx.enter_context(tc.psum_pool(name="ps", bufs=1))
+        ctx.enter_context(tc.manual_schedule())
+
+        def sbuf(name, shape, dtype):
+            return sb.tile(shape, dtype, name=name, align_bytes=64)
+
+        def cols(k):
+            return slice(k * CHUNK, (k + 1) * CHUNK)
+
+        operands = ["w1", "w2"] + [a + str(k) for a in ("x", "dx") for k in range(CHUNKS)]
+        raw = {o: sbuf(o + "_raw", [P, PACK, CHUNK], F32) for o in operands}
+        rounded = {o: sbuf(o + "_bf", [P, CHUNK, PACK], BF16) for o in operands}
+        codes = {o: sbuf(o + "_codes", [P, CHUNK], U32) for o in operands}
+        scales = {o: sbuf(o + "_scales", [P, CHUNK], U8) for o in operands}
+        base_sb = [sbuf("base%d" % g, [P, HALVES, N], F32) for g in range(G)]
+        factors = sbuf("factors", [P, 2, 8], F32)
+        halved = sbuf("halved", [P, 2, 8], F32)
+        units = [(g, k) for k in range(CHUNKS) for g in range(G)]
+        work = {
+            (s, u): sbuf("%s_%d%d" % (s, u[0], u[1]), [P, HALVES * CHUNK], F32)
+            for s in ("z1", "diff", "tanh", "up", "down", "mix", "y")
+            for u in units
+        }
+        gathered = [sbuf("gathered%d" % k, [P, PACK, CHUNK], F32) for k in range(CHUNKS)]
+        y_bf = [sbuf("y_bf%d" % k, [P, CHUNK, PACK], BF16) for k in range(CHUNKS)]
+        y_codes = [sbuf("y_codes%d" % k, [P, CHUNK], U32) for k in range(CHUNKS)]
+        y_scales = sbuf("y_scales", [P, N], U8)
+        bank = {
+            (s, g): ps.tile([P, HALVES * CHUNK], F32, name="%s_bank%d" % (s, g))
+            for s in ("z1", "z2", "tz1", "tz2")
+            for g in range(G)
+        }
+
+        def load_operand(name, src):
+            nc.sync.dma_start(out=raw[name][:], in_=src.rearrange("g (p j) c -> (g p) j c", j=PACK))
+
+        def load_base(g):
+            nc.sync.dma_start(out=base_sb[g][:], in_=base[g].rearrange("(q h) n -> q h n", h=HALVES))
+
+        def load_factor(which, src):
+            nc.sync.dma_start(
+                out=factors[:, which, 0 : G * HALVES].rearrange("q (g h) -> q g h", h=HALVES),
+                in_=src.rearrange("g (q h) o -> q g (h o)", h=HALVES),
+            )
+
+        def halve_factor(which):
+            nc.gpsimd.tensor_scalar(
+                out=halved[:, which, 0 : G * HALVES], in0=factors[:, which, 0 : G * HALVES], scalar1=0.5, scalar2=0.0,
+                op0=ALU.mult, op1=ALU.add,
+            )
+
+        def round_weights(name, vec_pairs):
+            dst = rounded[name][:].rearrange("p (h a i) j -> p a h (i j)", h=HALVES, i=2)
+            src = raw[name][:].rearrange("p j (a i h) -> p a h i j", h=HALVES, i=2)
+            nc.vector.tensor_copy(
+                out=dst[:, 0:vec_pairs].rearrange("p a h (i j) -> p a h i j", i=2), in_=src[:, 0:vec_pairs]
+            )
+            if vec_pairs < P // 2:
+                nc.scalar.copy(
+                    out=dst[:, vec_pairs : P // 2].rearrange("p a h (i j) -> p a h i j", i=2), in_=src[:, vec_pairs : P // 2]
+                )
+
+        def interleave(dst, src, vec_cols):
+            view = src[:].rearrange("p j c -> p c j")
+            if vec_cols > 0:
+                nc.vector.tensor_copy(out=dst[:, 0:vec_cols, :], in_=view[:, 0:vec_cols, :])
+            nc.scalar.activation(out=dst[:, vec_cols:CHUNK, :], in_=view[:, vec_cols:CHUNK, :], func=ACT.Copy)
+
+        def quantise(words, plane, src):
+            nc.vector.quantize_mx(out=words.bitcast(FP8X4), scales=plane, in_=src[:].rearrange("p c j -> p (c j)"))
+
+        def quantise_operand(name):
+            quantise(codes[name][:], scales[name][:], rounded[name])
+
+        def products(results, moving):
+            for result, weights in results:
+                for h in range(HALVES):
+                    for n0 in range(0, CHUNK, MM_N):
+                        for g in range(G):
+                            rows = slice(g * ROWS, (g + 1) * ROWS)
+                            m_cols = slice(h * P, (h + 1) * P)
+                            n_cols = slice(n0, n0 + MM_N)
+                            nc.tensor.matmul_mx(
+                                out=bank[result, g][:, h * CHUNK + n0 : h * CHUNK + n0 + MM_N],
+                                lhsT=codes[weights][rows, m_cols].bitcast(FP8X4),
+                                lhsT_scale=scales[weights][rows, m_cols],
+                                rhs=codes[moving][rows, n_cols].bitcast(FP8X4),
+                                rhs_scale=scales[moving][rows, n_cols],
+                                start=True,
+                                stop=True,
+                            )
+
+        def half(t, h):
+            return t[:, h * CHUNK : (h + 1) * CHUNK]
+
+        def factor(which, g, h):
+            return halved[:, which, g * HALVES + h : g * HALVES + h + 1]
+
+        def copy_z1(u):
+            nc.scalar.copy(out=work["z1", u][:], in_=bank["z1", u[0]][:])
+
+        def diff(u):
+            nc.vector.tensor_tensor(out=work["diff", u][:], in0=work["z1", u][:], in1=bank["z2", u[0]][:], op=ALU.subtract)
+
+        def tanh(u):
+            for h in range(HALVES):
+                nc.scalar.activation(
+                    out=half(work["tanh", u], h), in_=half(work["diff", u], h), func=ACT.Tanh, scale=factor(0, u[0], h)
+                )
+
+        def up(u):
+            nc.vector.scalar_tensor_tensor(
+                out=work["up", u][:], in0=work["tanh", u][:], scalar=1.0, in1=bank["tz1", u[0]][:], op0=ALU.add, op1=ALU.mult
+            )
+
+        def down(u):
+            nc.vector.scalar_tensor_tensor(
+                out=work["down", u][:], in0=work["tanh", u][:], scalar=1.0, in1=bank["tz2", u[0]][:], op0=ALU.subtract, op1=ALU.mult
+            )
+
+        def mix(u, part):
+            nc.vector.tensor_tensor(out=work["mix", u][:, part], in0=work["up", u][:, part], in1=work["down", u][:, part], op=ALU.subtract)
+
+        whole = slice(0, HALVES * CHUNK)
+
+        def finish(u):
+            g, k = u
+            y = work["y", u]
+            for h in range(HALVES):
+                nc.vector.scalar_tensor_tensor(
+                    out=half(y, h), in0=half(work["mix", u], h), scalar=factor(1, g, h), in1=base_sb[g][:, h, cols(k)],
+                    op0=ALU.mult, op1=ALU.add,
+                )
+            nc.sync.dma_start(
+                out=gathered[k][g * ROWS : (g + 1) * ROWS].rearrange("s (a h) c -> s a (h c)", h=HALVES), in_=y[:]
+            )
+            nc.sync.dma_start(
+                out=out_0[g * M : (g + 1) * M, cols(k)].rearrange("(q h) c -> q h c", h=HALVES),
+                in_=y[:].rearrange("q (h c) -> q h c", h=HALVES),
+            )
+
+        words_out = out_1.rearrange("s p n u -> (s p) (n u)").bitcast(I32)
+
+        def planes(k):
+            quantise(y_codes[k][:], y_scales[:, cols(k)], y_bf[k])
+            nc.sync.dma_start(out=words_out[:, cols(k)], in_=y_codes[k][:].bitcast(I32))
+
+        load_operand("w1", w1)
+        load_operand("x0", x[:, :, cols(0)])
+        load_operand("w2", w2)
+        load_operand("dx0", dx[:, :, cols(0)])
+        load_factor(0, tp)
+        load_base(0)
+        load_factor(1, og)
+        load_operand("x1", x[:, :, cols(1)])
+        load_base(1)
+        load_operand("dx1", dx[:, :, cols(1)])
+        halve_factor(0)
+        halve_factor(1)
+
+        a0, b0, a1, b1 = units
+        round_weights("w1", P // 2)
+        quantise_operand("w1")
+        interleave(rounded["x0"], raw["x0"], VEC_COLS)
+        quantise_operand("x0")
+        products([("z1", "w1")], "x0")
+        round_weights("w2", VEC_COLS // 4)
+        quantise_operand("w2")
+        products([("z2", "w2")], "x0")
+        copy_z1(a0)
+        interleave(rounded["dx0"], raw["dx0"], VEC_COLS)
+        quantise_operand("dx0")
+        products([("tz1", "w1"), ("tz2", "w2")], "dx0")
+
+        copy_z1(b0)
+        diff(a0)
+        tanh(a0)
+        diff(b0)
+        tanh(b0)
+        interleave(rounded["x1"], raw["x1"], 0)
+        interleave(rounded["dx1"], raw["dx1"], 0)
+        up(a0)
+        down(a0)
+        up(b0)
+        mix(a0, whole)
+        down(b0)
+        quantise_operand("x1")
+        products([("z1", "w1"), ("z2", "w2")], "x1")
+        finish(a0)
+        mix(b0, whole)
+        quantise_operand("dx1")
+        products([("tz1", "w1"), ("tz2", "w2")], "dx1")
+        copy_z1(a1)
+        copy_z1(b1)
+        diff(a1)
+        tanh(a1)
+        finish(b0)
+        diff(b1)
+        tanh(b1)
+        interleave(y_bf[0], gathered[0], 0)
+        up(a1)
+        down(a1)
+        up(b1)
+        mix(a1, whole)
+        down(b1)
+        finish(a1)
+        for h in range(HALVES):
+            mix(b1, slice(h * CHUNK, (h + 1) * CHUNK))
+        finish(b1)
+        planes(0)
+        interleave(y_bf[1], gathered[1], VEC_COLS)
+        planes(1)
+        for quad in range(4):
+            queue = nc.scalar if quad % 2 else nc.sync
+            queue.dma_start(
+                out=out_2[0, 4 * quad : 4 * quad + 4, :].bitcast(I32),
+                in_=y_scales[32 * quad : 32 * quad + 4, :].bitcast(I32),
+            )

@@ -22,6 +22,7 @@ CHUNK = 256
 CHUNKS = N // CHUNK
 MM_N = 128
 VEC_COLS = 176
+STRIPS = [(0, 256), (256, 128), (384, 128)]
 
 
 def tile_rows_pl_tnsoftmaxoftwo_kernel(tc, x, w1, w2, tp, dx, og, base, out_0, out_1, out_2):
@@ -44,16 +45,17 @@ def tile_rows_pl_tnsoftmaxoftwo_kernel(tc, x, w1, w2, tp, dx, og, base, out_0, o
         scales = {o: sbuf(o + "_scales", [P, CHUNK], U8) for o in operands}
         base_sb = [sbuf("base%d" % g, [P, HALVES, N], F32) for g in range(G)]
         factors = sbuf("factors", [P, 2, 8], F32)
-        halved = sbuf("halved", [P, 2, 8], F32)
+        half_gain = sbuf("half_gain", [P, G * HALVES], F32)
         units = [(g, k) for k in range(CHUNKS) for g in range(G)]
         work = {
             (s, u): sbuf("%s_%d%d" % (s, u[0], u[1]), [P, HALVES * CHUNK], F32)
-            for s in ("z1", "diff", "tanh", "up", "down", "mix", "y")
+            for s in ("z1", "diff", "tanh", "up", "down", "mix")
             for u in units
         }
-        gathered = [sbuf("gathered%d" % k, [P, PACK, CHUNK], F32) for k in range(CHUNKS)]
-        y_bf = [sbuf("y_bf%d" % k, [P, CHUNK, PACK], BF16) for k in range(CHUNKS)]
-        y_codes = [sbuf("y_codes%d" % k, [P, CHUNK], U32) for k in range(CHUNKS)]
+        y = {(g, n0): sbuf("y%d_%d" % (g, n0), [P, HALVES, w], F32) for g in range(G) for n0, w in STRIPS}
+        gathered = {n0: sbuf("gathered%d" % n0, [P, PACK, w], F32) for n0, w in STRIPS}
+        y_bf = {n0: sbuf("y_bf%d" % n0, [P, w, PACK], BF16) for n0, w in STRIPS}
+        y_codes = {n0: sbuf("y_codes%d" % n0, [P, w], U32) for n0, w in STRIPS}
         y_scales = sbuf("y_scales", [P, N], U8)
         bank = {
             (s, g): ps.tile([P, HALVES * CHUNK], F32, name="%s_bank%d" % (s, g))
@@ -67,16 +69,15 @@ def tile_rows_pl_tnsoftmaxoftwo_kernel(tc, x, w1, w2, tp, dx, og, base, out_0, o
         def load_base(g):
             nc.sync.dma_start(out=base_sb[g][:], in_=base[g].rearrange("(q h) n -> q h n", h=HALVES))
 
-        def load_factor(which, src):
-            nc.sync.dma_start(
+        def load_factor(queue, which, src):
+            queue.dma_start(
                 out=factors[:, which, 0 : G * HALVES].rearrange("q (g h) -> q g h", h=HALVES),
                 in_=src.rearrange("g (q h) o -> q g (h o)", h=HALVES),
             )
 
-        def halve_factor(which):
+        def halve_gain():
             nc.gpsimd.tensor_scalar(
-                out=halved[:, which, 0 : G * HALVES], in0=factors[:, which, 0 : G * HALVES], scalar1=0.5, scalar2=0.0,
-                op0=ALU.mult, op1=ALU.add,
+                out=half_gain[:], in0=factors[:, 1, 0 : G * HALVES], scalar1=0.5, scalar2=0.0, op0=ALU.mult, op1=ALU.add
             )
 
         def round_weights(name, vec_pairs):
@@ -92,9 +93,11 @@ def tile_rows_pl_tnsoftmaxoftwo_kernel(tc, x, w1, w2, tp, dx, og, base, out_0, o
 
         def interleave(dst, src, vec_cols):
             view = src[:].rearrange("p j c -> p c j")
+            width = src.shape[2]
             if vec_cols > 0:
                 nc.vector.tensor_copy(out=dst[:, 0:vec_cols, :], in_=view[:, 0:vec_cols, :])
-            nc.scalar.activation(out=dst[:, vec_cols:CHUNK, :], in_=view[:, vec_cols:CHUNK, :], func=ACT.Copy)
+            if vec_cols < width:
+                nc.scalar.activation(out=dst[:, vec_cols:width, :], in_=view[:, vec_cols:width, :], func=ACT.Copy)
 
         def quantise(words, plane, src):
             nc.vector.quantize_mx(out=words.bitcast(FP8X4), scales=plane, in_=src[:].rearrange("p c j -> p (c j)"))
@@ -102,40 +105,45 @@ def tile_rows_pl_tnsoftmaxoftwo_kernel(tc, x, w1, w2, tp, dx, og, base, out_0, o
         def quantise_operand(name):
             quantise(codes[name][:], scales[name][:], rounded[name])
 
+        def product(result, weights, moving, g):
+            rows = slice(g * ROWS, (g + 1) * ROWS)
+            for h in range(HALVES):
+                m_cols = slice(h * P, (h + 1) * P)
+                for n0 in range(0, CHUNK, MM_N):
+                    n_cols = slice(n0, n0 + MM_N)
+                    nc.tensor.matmul_mx(
+                        out=bank[result, g][:, h * CHUNK + n0 : h * CHUNK + n0 + MM_N],
+                        lhsT=codes[weights][rows, m_cols].bitcast(FP8X4),
+                        lhsT_scale=scales[weights][rows, m_cols],
+                        rhs=codes[moving][rows, n_cols].bitcast(FP8X4),
+                        rhs_scale=scales[moving][rows, n_cols],
+                        start=True,
+                        stop=True,
+                    )
+
         def products(results, moving):
-            for result, weights in results:
-                for h in range(HALVES):
-                    for n0 in range(0, CHUNK, MM_N):
-                        for g in range(G):
-                            rows = slice(g * ROWS, (g + 1) * ROWS)
-                            m_cols = slice(h * P, (h + 1) * P)
-                            n_cols = slice(n0, n0 + MM_N)
-                            nc.tensor.matmul_mx(
-                                out=bank[result, g][:, h * CHUNK + n0 : h * CHUNK + n0 + MM_N],
-                                lhsT=codes[weights][rows, m_cols].bitcast(FP8X4),
-                                lhsT_scale=scales[weights][rows, m_cols],
-                                rhs=codes[moving][rows, n_cols].bitcast(FP8X4),
-                                rhs_scale=scales[moving][rows, n_cols],
-                                start=True,
-                                stop=True,
-                            )
+            for g in range(G):
+                for result, weights in results:
+                    product(result, weights, moving, g)
 
         def half(t, h):
             return t[:, h * CHUNK : (h + 1) * CHUNK]
 
-        def factor(which, g, h):
-            return halved[:, which, g * HALVES + h : g * HALVES + h + 1]
+        def column(t, g, h):
+            return t[:, g * HALVES + h : g * HALVES + h + 1]
 
         def copy_z1(u):
-            nc.scalar.copy(out=work["z1", u][:], in_=bank["z1", u[0]][:])
+            nc.scalar.activation(out=work["z1", u][:], in_=bank["z1", u[0]][:], func=ACT.Copy, scale=0.5)
 
         def diff(u):
-            nc.vector.tensor_tensor(out=work["diff", u][:], in0=work["z1", u][:], in1=bank["z2", u[0]][:], op=ALU.subtract)
+            nc.vector.scalar_tensor_tensor(
+                out=work["diff", u][:], in0=bank["z2", u[0]][:], scalar=-0.5, in1=work["z1", u][:], op0=ALU.mult, op1=ALU.add
+            )
 
         def tanh(u):
             for h in range(HALVES):
                 nc.scalar.activation(
-                    out=half(work["tanh", u], h), in_=half(work["diff", u], h), func=ACT.Tanh, scale=factor(0, u[0], h)
+                    out=half(work["tanh", u], h), in_=half(work["diff", u], h), func=ACT.Tanh, scale=column(factors[:, 0, :], u[0], h)
                 )
 
         def up(u):
@@ -148,47 +156,57 @@ def tile_rows_pl_tnsoftmaxoftwo_kernel(tc, x, w1, w2, tp, dx, og, base, out_0, o
                 out=work["down", u][:], in0=work["tanh", u][:], scalar=1.0, in1=bank["tz2", u[0]][:], op0=ALU.subtract, op1=ALU.mult
             )
 
-        def mix(u, part):
-            nc.vector.tensor_tensor(out=work["mix", u][:, part], in0=work["up", u][:, part], in1=work["down", u][:, part], op=ALU.subtract)
+        def strip_of(name, u, strip):
+            n0, w = strip
+            first = n0 - u[1] * CHUNK
+            return work[name, u][:].rearrange("q (h c) -> q h c", h=HALVES)[:, :, first : first + w]
 
-        whole = slice(0, HALVES * CHUNK)
+        def mix(engine, u, strip):
+            engine.tensor_tensor(
+                out=strip_of("mix", u, strip), in0=strip_of("up", u, strip), in1=strip_of("down", u, strip), op=ALU.subtract
+            )
 
-        def finish(u):
-            g, k = u
-            y = work["y", u]
+        def finish(u, strip):
+            g = u[0]
+            n0, w = strip
             for h in range(HALVES):
                 nc.vector.scalar_tensor_tensor(
-                    out=half(y, h), in0=half(work["mix", u], h), scalar=factor(1, g, h), in1=base_sb[g][:, h, cols(k)],
-                    op0=ALU.mult, op1=ALU.add,
+                    out=y[g, n0][:, h, :], in0=strip_of("mix", u, strip)[:, h, :], scalar=column(half_gain, g, h),
+                    in1=base_sb[g][:, h, n0 : n0 + w], op0=ALU.mult, op1=ALU.add,
                 )
             nc.sync.dma_start(
-                out=gathered[k][g * ROWS : (g + 1) * ROWS].rearrange("s (a h) c -> s a (h c)", h=HALVES), in_=y[:]
+                out=gathered[n0][g * ROWS : (g + 1) * ROWS].rearrange("s (a h) c -> s a (h c)", h=HALVES),
+                in_=y[g, n0][:].rearrange("q h c -> q (h c)"),
             )
-            nc.sync.dma_start(
-                out=out_0[g * M : (g + 1) * M, cols(k)].rearrange("(q h) c -> q h c", h=HALVES),
-                in_=y[:].rearrange("q (h c) -> q h c", h=HALVES),
+
+        def store_y(queue, g, strip):
+            n0, w = strip
+            queue.dma_start(
+                out=out_0[g * M : (g + 1) * M, n0 : n0 + w].rearrange("(q h) c -> q h c", h=HALVES), in_=y[g, n0][:]
             )
 
         words_out = out_1.rearrange("s p n u -> (s p) (n u)").bitcast(I32)
 
-        def planes(k):
-            quantise(y_codes[k][:], y_scales[:, cols(k)], y_bf[k])
-            nc.sync.dma_start(out=words_out[:, cols(k)], in_=y_codes[k][:].bitcast(I32))
+        def planes(strip):
+            n0, w = strip
+            quantise(y_codes[n0][:], y_scales[:, n0 : n0 + w], y_bf[n0])
+            nc.sync.dma_start(out=words_out[:, n0 : n0 + w], in_=y_codes[n0][:].bitcast(I32))
 
+        load_factor(nc.scalar, 0, tp)
         load_operand("w1", w1)
         load_operand("x0", x[:, :, cols(0)])
         load_operand("w2", w2)
         load_operand("dx0", dx[:, :, cols(0)])
-        load_factor(0, tp)
-        load_base(0)
-        load_factor(1, og)
         load_operand("x1", x[:, :, cols(1)])
-        load_base(1)
         load_operand("dx1", dx[:, :, cols(1)])
-        halve_factor(0)
-        halve_factor(1)
+        load_factor(nc.sync, 1, og)
+        load_base(0)
+        load_base(1)
+        halve_gain()
 
         a0, b0, a1, b1 = units
+        first, second, last = STRIPS
+        both = (second[0], CHUNK)
         round_weights("w1", P // 2)
         quantise_operand("w1")
         interleave(rounded["x0"], raw["x0"], VEC_COLS)
@@ -198,12 +216,11 @@ def tile_rows_pl_tnsoftmaxoftwo_kernel(tc, x, w1, w2, tp, dx, og, base, out_0, o
         quantise_operand("w2")
         products([("z2", "w2")], "x0")
         copy_z1(a0)
+        copy_z1(b0)
         interleave(rounded["dx0"], raw["dx0"], VEC_COLS)
+        diff(a0)
         quantise_operand("dx0")
         products([("tz1", "w1"), ("tz2", "w2")], "dx0")
-
-        copy_z1(b0)
-        diff(a0)
         tanh(a0)
         diff(b0)
         tanh(b0)
@@ -212,34 +229,44 @@ def tile_rows_pl_tnsoftmaxoftwo_kernel(tc, x, w1, w2, tp, dx, og, base, out_0, o
         up(a0)
         down(a0)
         up(b0)
-        mix(a0, whole)
-        down(b0)
+        mix(nc.vector, a0, first)
         quantise_operand("x1")
         products([("z1", "w1"), ("z2", "w2")], "x1")
-        finish(a0)
-        mix(b0, whole)
+        down(b0)
+        finish(a0, first)
+        store_y(nc.sync, 0, first)
+        mix(nc.vector, b0, first)
         quantise_operand("dx1")
         products([("tz1", "w1"), ("tz2", "w2")], "dx1")
         copy_z1(a1)
         copy_z1(b1)
         diff(a1)
         tanh(a1)
-        finish(b0)
+        finish(b0, first)
+        store_y(nc.sync, 1, first)
         diff(b1)
         tanh(b1)
-        interleave(y_bf[0], gathered[0], 0)
+        interleave(y_bf[first[0]], gathered[first[0]], 0)
         up(a1)
         down(a1)
         up(b1)
-        mix(a1, whole)
+        mix(nc.vector, a1, both)
         down(b1)
-        finish(a1)
-        for h in range(HALVES):
-            mix(b1, slice(h * CHUNK, (h + 1) * CHUNK))
-        finish(b1)
-        planes(0)
-        interleave(y_bf[1], gathered[1], VEC_COLS)
-        planes(1)
+        finish(a1, second)
+        mix(nc.vector, b1, second)
+        mix(nc.vector, b1, last)
+        finish(b1, second)
+        finish(a1, last)
+        finish(b1, last)
+        planes(first)
+        for g in range(G):
+            store_y(nc.scalar, g, second)
+        interleave(y_bf[second[0]], gathered[second[0]], 0)
+        for g in range(G):
+            store_y(nc.scalar, g, last)
+        interleave(y_bf[last[0]], gathered[last[0]], last[1])
+        planes(second)
+        planes(last)
         for quad in range(4):
             queue = nc.scalar if quad % 2 else nc.sync
             queue.dma_start(

@@ -22,7 +22,8 @@ CHUNK = 256
 CHUNKS = N // CHUNK
 MM_N = 128
 VEC_COLS = 176
-STRIPS = [(0, 256), (256, 128), (384, 128)]
+BANK = HALVES * CHUNK
+SPREAD = (2 * PACK + 1) * ROWS
 
 
 def tile_rows_pl_tnsoftmaxoftwo_kernel(tc, x, w1, w2, tp, dx, og, base, out_0, out_1, out_2):
@@ -38,27 +39,40 @@ def tile_rows_pl_tnsoftmaxoftwo_kernel(tc, x, w1, w2, tp, dx, og, base, out_0, o
         def cols(k):
             return slice(k * CHUNK, (k + 1) * CHUNK)
 
-        operands = ["w1", "w2"] + [a + str(k) for a in ("x", "dx") for k in range(CHUNKS)]
+        def rows(i):
+            return slice(i * ROWS, (i + 1) * ROWS)
+
+        def strip(k, c):
+            return slice(k * CHUNK + c * MM_N, k * CHUNK + (c + 1) * MM_N)
+
+        weights = ("w1", "w2")
+        operands = list(weights) + [a + str(k) for a in ("x", "dx") for k in range(CHUNKS)]
         raw = {o: sbuf(o + "_raw", [P, PACK, CHUNK], F32) for o in operands}
         rounded = {o: sbuf(o + "_bf", [P, CHUNK, PACK], BF16) for o in operands}
         codes = {o: sbuf(o + "_codes", [P, CHUNK], U32) for o in operands}
         scales = {o: sbuf(o + "_scales", [P, CHUNK], U8) for o in operands}
-        base_sb = [sbuf("base%d" % g, [P, HALVES, N], F32) for g in range(G)]
-        factors = sbuf("factors", [P, 2, 8], F32)
-        half_gain = sbuf("half_gain", [P, G * HALVES], F32)
+        spread_codes = {w: sbuf(w + "_spread_codes", [P, SPREAD], U32) for w in weights}
+        spread_scales = {w: sbuf(w + "_spread_scales", [P, SPREAD], U8) for w in weights}
         units = [(g, k) for k in range(CHUNKS) for g in range(G)]
+        a0, b0, a1, b1 = units
+        base_0 = sbuf("base_0", [P, HALVES, N], F32)
+        base_b0 = sbuf("base_b0", [P, HALVES, CHUNK], F32)
+        base_b1 = sbuf("base_b1", [P, PACK, MM_N], F32)
+        factors = sbuf("factors", [P, 2, 8], F32)
+        factors_b1 = sbuf("factors_b1", [P, 2, 8], F32)
+        half_gain = sbuf("half_gain", [P, PACK], F32)
+        half_gain_b1 = sbuf("half_gain_b1", [P, PACK], F32)
         work = {
-            (s, u): sbuf("%s_%d%d" % (s, u[0], u[1]), [P, HALVES * CHUNK], F32)
-            for s in ("z1", "diff", "tanh", "up", "down", "mix")
+            (s, u): sbuf("%s_%d%d" % (s, u[0], u[1]), [P, BANK], F32)
+            for s in ("z1", "diff", "tanh", "up", "down", "mix", "y")
             for u in units
         }
-        y = {(g, n0): sbuf("y%d_%d" % (g, n0), [P, HALVES, w], F32) for g in range(G) for n0, w in STRIPS}
-        gathered = {n0: sbuf("gathered%d" % n0, [P, PACK, w], F32) for n0, w in STRIPS}
-        y_bf = {n0: sbuf("y_bf%d" % n0, [P, w, PACK], BF16) for n0, w in STRIPS}
-        y_codes = {n0: sbuf("y_codes%d" % n0, [P, w], U32) for n0, w in STRIPS}
-        y_scales = sbuf("y_scales", [P, N], U8)
+        gathered = {u: sbuf("gathered_%d%d" % u, [P, PACK, MM_N], F32) for u in (a0, b0, a1)}
+        y_bf = {u: sbuf("y_bf_%d%d" % u, [P, MM_N, PACK], BF16) for u in units}
+        y_codes = [sbuf("y_codes%d" % k, [P, CHUNK], U32) for k in range(CHUNKS)]
+        y_scales = [sbuf("y_scales%d" % k, [P, CHUNK], U8) for k in range(CHUNKS)]
         bank = {
-            (s, g): ps.tile([P, HALVES * CHUNK], F32, name="%s_bank%d" % (s, g))
+            (s, g): ps.tile([P, BANK], F32, name="%s_bank%d" % (s, g))
             for s in ("z1", "z2", "tz1", "tz2")
             for g in range(G)
         }
@@ -66,38 +80,36 @@ def tile_rows_pl_tnsoftmaxoftwo_kernel(tc, x, w1, w2, tp, dx, og, base, out_0, o
         def load_operand(name, src):
             nc.sync.dma_start(out=raw[name][:], in_=src.rearrange("g (p j) c -> (g p) j c", j=PACK))
 
-        def load_base(g):
-            nc.sync.dma_start(out=base_sb[g][:], in_=base[g].rearrange("(q h) n -> q h n", h=HALVES))
-
         def load_factor(queue, which, src):
             queue.dma_start(
                 out=factors[:, which, 0 : G * HALVES].rearrange("q (g h) -> q g h", h=HALVES),
                 in_=src.rearrange("g (q h) o -> q g (h o)", h=HALVES),
             )
 
-        def halve_gain():
-            nc.gpsimd.tensor_scalar(
-                out=half_gain[:], in0=factors[:, 1, 0 : G * HALVES], scalar1=0.5, scalar2=0.0, op0=ALU.mult, op1=ALU.add
-            )
+        def halve(dst, src):
+            nc.gpsimd.tensor_scalar(out=dst[:], in0=src[:, 1, 0:PACK], scalar1=0.5, scalar2=0.0, op0=ALU.mult, op1=ALU.add)
 
         def round_weights(name, vec_pairs):
-            dst = rounded[name][:].rearrange("p (h a i) j -> p a h (i j)", h=HALVES, i=2)
+            dst = rounded[name][:].rearrange("p (h a i) j -> p a h i j", h=HALVES, i=2)
             src = raw[name][:].rearrange("p j (a i h) -> p a h i j", h=HALVES, i=2)
-            nc.vector.tensor_copy(
-                out=dst[:, 0:vec_pairs].rearrange("p a h (i j) -> p a h i j", i=2), in_=src[:, 0:vec_pairs]
-            )
+            nc.vector.tensor_copy(out=dst[:, 0:vec_pairs], in_=src[:, 0:vec_pairs])
             if vec_pairs < P // 2:
-                nc.scalar.copy(
-                    out=dst[:, vec_pairs : P // 2].rearrange("p a h (i j) -> p a h i j", i=2), in_=src[:, vec_pairs : P // 2]
+                nc.scalar.copy(out=dst[:, vec_pairs : P // 2], in_=src[:, vec_pairs : P // 2])
+
+        def interleave_vector(dst, src, stop):
+            nc.vector.tensor_copy(out=dst[:, 0:stop, :], in_=src[:].rearrange("p j c -> p c j")[:, 0:stop, :])
+
+        def interleave_scalar(dst, src, start):
+            width = src.shape[2]
+            if start < width:
+                nc.scalar.activation(
+                    out=dst[:, start:width, :], in_=src[:].rearrange("p j c -> p c j")[:, start:width, :], func=ACT.Copy
                 )
 
         def interleave(dst, src, vec_cols):
-            view = src[:].rearrange("p j c -> p c j")
-            width = src.shape[2]
             if vec_cols > 0:
-                nc.vector.tensor_copy(out=dst[:, 0:vec_cols, :], in_=view[:, 0:vec_cols, :])
-            if vec_cols < width:
-                nc.scalar.activation(out=dst[:, vec_cols:width, :], in_=view[:, vec_cols:width, :], func=ACT.Copy)
+                interleave_vector(dst, src, vec_cols)
+            interleave_scalar(dst, src, vec_cols)
 
         def quantise(words, plane, src):
             nc.vector.quantize_mx(out=words.bitcast(FP8X4), scales=plane, in_=src[:].rearrange("p c j -> p (c j)"))
@@ -105,171 +117,248 @@ def tile_rows_pl_tnsoftmaxoftwo_kernel(tc, x, w1, w2, tp, dx, og, base, out_0, o
         def quantise_operand(name):
             quantise(codes[name][:], scales[name][:], rounded[name])
 
-        def product(result, weights, moving, g):
-            rows = slice(g * ROWS, (g + 1) * ROWS)
+        def spread_views(dst, src):
+            return (
+                dst[:, ROWS:SPREAD].rearrange("p (a h z s) -> p a h z s", a=2, h=HALVES, z=2)[:, :, :, 0, :],
+                src.rearrange("p (h s a) -> p a h s", h=HALVES, a=2),
+            )
+
+        def matmul(out, w_codes, w_scales, moving, g, n0, start, stop):
+            n_cols = slice(n0, n0 + MM_N)
+            nc.tensor.matmul_mx(
+                out=out,
+                lhsT=w_codes.bitcast(FP8X4),
+                lhsT_scale=w_scales,
+                rhs=codes[moving][rows(g), n_cols].bitcast(FP8X4),
+                rhs_scale=scales[moving][rows(g), n_cols],
+                start=start,
+                stop=stop,
+            )
+
+        def product(result, w, moving, g):
             for h in range(HALVES):
                 m_cols = slice(h * P, (h + 1) * P)
                 for n0 in range(0, CHUNK, MM_N):
-                    n_cols = slice(n0, n0 + MM_N)
-                    nc.tensor.matmul_mx(
-                        out=bank[result, g][:, h * CHUNK + n0 : h * CHUNK + n0 + MM_N],
-                        lhsT=codes[weights][rows, m_cols].bitcast(FP8X4),
-                        lhsT_scale=scales[weights][rows, m_cols],
-                        rhs=codes[moving][rows, n_cols].bitcast(FP8X4),
-                        rhs_scale=scales[moving][rows, n_cols],
-                        start=True,
-                        stop=True,
+                    out = bank[result, g][:, h * CHUNK + n0 : h * CHUNK + n0 + MM_N]
+                    matmul(out, codes[w][rows(g), m_cols], scales[w][rows(g), m_cols], moving, g, n0, True, True)
+
+        def spread_product(result, w, moving):
+            for t in range(PACK):
+                out = bank[result, 1][:, t * MM_N : (t + 1) * MM_N]
+                for c in range(2):
+                    m_cols = slice((2 * t + 1 - c) * ROWS, (2 * t + 1 - c) * ROWS + P)
+                    matmul(
+                        out, spread_codes[w][rows(1), m_cols], spread_scales[w][rows(1), m_cols], moving, 1, c * MM_N,
+                        c == 0, c == 1,
                     )
 
-        def products(results, moving):
-            for g in range(G):
-                for result, weights in results:
-                    product(result, weights, moving, g)
+        whole = slice(0, BANK)
+        low, high = slice(0, BANK // 2), slice(BANK // 2, BANK)
 
-        def half(t, h):
-            return t[:, h * CHUNK : (h + 1) * CHUNK]
-
-        def column(t, g, h):
-            return t[:, g * HALVES + h : g * HALVES + h + 1]
+        def pieces(u, part):
+            if u == b1:
+                return [(slice(n0, n0 + MM_N), n0 // MM_N) for n0 in range(part.start, part.stop, MM_N)]
+            return [(slice(n0, n0 + CHUNK), u[0] * HALVES + n0 // CHUNK) for n0 in range(part.start, part.stop, CHUNK)]
 
         def copy_z1(u):
             nc.scalar.activation(out=work["z1", u][:], in_=bank["z1", u[0]][:], func=ACT.Copy, scale=0.5)
 
-        def diff(u):
+        def diff(u, part):
             nc.vector.scalar_tensor_tensor(
-                out=work["diff", u][:], in0=bank["z2", u[0]][:], scalar=-0.5, in1=work["z1", u][:], op0=ALU.mult, op1=ALU.add
+                out=work["diff", u][:, part], in0=bank["z2", u[0]][:, part], scalar=-0.5, in1=work["z1", u][:, part],
+                op0=ALU.mult, op1=ALU.add,
             )
 
-        def tanh(u):
-            for h in range(HALVES):
+        def tanh(u, part):
+            temper = factors_b1 if u == b1 else factors
+            for piece, i in pieces(u, part):
                 nc.scalar.activation(
-                    out=half(work["tanh", u], h), in_=half(work["diff", u], h), func=ACT.Tanh, scale=column(factors[:, 0, :], u[0], h)
+                    out=work["tanh", u][:, piece], in_=work["diff", u][:, piece], func=ACT.Tanh, scale=temper[:, 0, i : i + 1]
                 )
 
-        def up(u):
+        def up(u, part):
             nc.vector.scalar_tensor_tensor(
-                out=work["up", u][:], in0=work["tanh", u][:], scalar=1.0, in1=bank["tz1", u[0]][:], op0=ALU.add, op1=ALU.mult
+                out=work["up", u][:, part], in0=work["tanh", u][:, part], scalar=1.0, in1=bank["tz1", u[0]][:, part],
+                op0=ALU.add, op1=ALU.mult,
             )
 
-        def down(u):
+        def down(u, part):
             nc.vector.scalar_tensor_tensor(
-                out=work["down", u][:], in0=work["tanh", u][:], scalar=1.0, in1=bank["tz2", u[0]][:], op0=ALU.subtract, op1=ALU.mult
+                out=work["down", u][:, part], in0=work["tanh", u][:, part], scalar=1.0, in1=bank["tz2", u[0]][:, part],
+                op0=ALU.subtract, op1=ALU.mult,
             )
 
-        def strip_of(name, u, strip):
-            n0, w = strip
-            first = n0 - u[1] * CHUNK
-            return work[name, u][:].rearrange("q (h c) -> q h c", h=HALVES)[:, :, first : first + w]
-
-        def mix(engine, u, strip):
+        def mix(engine, u, part):
             engine.tensor_tensor(
-                out=strip_of("mix", u, strip), in0=strip_of("up", u, strip), in1=strip_of("down", u, strip), op=ALU.subtract
+                out=work["mix", u][:, part], in0=work["up", u][:, part], in1=work["down", u][:, part], op=ALU.subtract
             )
 
-        def finish(u, strip):
-            g = u[0]
-            n0, w = strip
-            for h in range(HALVES):
+        def base_of(u, i):
+            if u == b1:
+                return base_b1[:, i, :]
+            if u == b0:
+                return base_b0[:, i - HALVES, :]
+            return base_0[:, i, cols(u[1])]
+
+        def finish(u, part):
+            gain = half_gain_b1 if u == b1 else half_gain
+            for piece, i in pieces(u, part):
                 nc.vector.scalar_tensor_tensor(
-                    out=y[g, n0][:, h, :], in0=strip_of("mix", u, strip)[:, h, :], scalar=column(half_gain, g, h),
-                    in1=base_sb[g][:, h, n0 : n0 + w], op0=ALU.mult, op1=ALU.add,
+                    out=work["y", u][:, piece], in0=work["mix", u][:, piece], scalar=gain[:, i : i + 1], in1=base_of(u, i),
+                    op0=ALU.mult, op1=ALU.add,
                 )
+
+        def store_y(u):
+            g, k = u
             nc.sync.dma_start(
-                out=gathered[n0][g * ROWS : (g + 1) * ROWS].rearrange("s (a h) c -> s a (h c)", h=HALVES),
-                in_=y[g, n0][:].rearrange("q h c -> q (h c)"),
+                out=out_0[g * M : (g + 1) * M, cols(k)].rearrange("(q h) c -> q h c", h=HALVES),
+                in_=work["y", u][:].rearrange("q (h c) -> q h c", h=HALVES),
             )
 
-        def store_y(queue, g, strip):
-            n0, w = strip
-            queue.dma_start(
-                out=out_0[g * M : (g + 1) * M, n0 : n0 + w].rearrange("(q h) c -> q h c", h=HALVES), in_=y[g, n0][:]
-            )
+        def gather(u):
+            y = work["y", u][:].rearrange("q (h c) -> q h c", h=HALVES)
+            for c in range(2):
+                nc.sync.dma_start(out=gathered[u][rows(c)], in_=y[:, :, c * MM_N : (c + 1) * MM_N])
+
+        def quantise_y(u):
+            g, k = u
+            window = slice(g * MM_N, (g + 1) * MM_N)
+            quantise(y_codes[k][:, window], y_scales[k][:, window], y_bf[u])
 
         words_out = out_1.rearrange("s p n u -> (s p) (n u)").bitcast(I32)
 
-        def planes(strip):
-            n0, w = strip
-            quantise(y_codes[n0][:], y_scales[:, n0 : n0 + w], y_bf[n0])
-            nc.sync.dma_start(out=words_out[:, n0 : n0 + w], in_=y_codes[n0][:].bitcast(I32))
+        def store_words(queue, k, c):
+            queue.dma_start(
+                out=words_out[:, strip(k, c)].rearrange("(g s) j -> s g j", g=G),
+                in_=y_codes[k][rows(c), :].bitcast(I32).rearrange("s (g j) -> s g j", g=G),
+            )
 
-        load_factor(nc.scalar, 0, tp)
+        def store_scales(queue, k, quad):
+            first_row = 4 * (quad % 2)
+            queue.dma_start(
+                out=out_2[0, :, strip(k, quad // 2)].bitcast(I32).rearrange("(g f) j -> f g j", g=G)[first_row : first_row + 4],
+                in_=y_scales[k][32 * quad : 32 * quad + 4, :].bitcast(I32).rearrange("r (g j) -> r g j", g=G),
+            )
+
+        for w in weights:
+            nc.gpsimd.memset(scales[w][:].bitcast(U32), 0)
+        for w in weights:
+            nc.gpsimd.memset(spread_scales[w][:].bitcast(U32), 0)
+            nc.gpsimd.memset(spread_codes[w][rows(1), :], 0)
+
         load_operand("w1", w1)
         load_operand("x0", x[:, :, cols(0)])
         load_operand("w2", w2)
         load_operand("dx0", dx[:, :, cols(0)])
+        load_factor(nc.sync, 0, tp)
         load_operand("x1", x[:, :, cols(1)])
         load_operand("dx1", dx[:, :, cols(1)])
         load_factor(nc.sync, 1, og)
-        load_base(0)
-        load_base(1)
-        halve_gain()
+        nc.sync.dma_start(out=base_0[:], in_=base[0].rearrange("(q h) n -> q h n", h=HALVES))
+        nc.sync.dma_start(out=base_b0[:], in_=base[1, :, cols(0)].rearrange("(q h) n -> q h n", h=HALVES))
+        for c in range(2):
+            for which, src in enumerate((tp, og)):
+                nc.sync.dma_start(
+                    out=factors_b1[rows(c), which, 0:PACK], in_=src[1].rearrange("(s t) o -> s (t o)", t=PACK)
+                )
+            nc.sync.dma_start(out=base_b1[rows(c)], in_=base[1, :, strip(1, c)].rearrange("(s t) n -> s t n", t=PACK))
 
-        a0, b0, a1, b1 = units
-        first, second, last = STRIPS
-        both = (second[0], CHUNK)
-        round_weights("w1", P // 2)
+        def spread_words(w):
+            dst, src = spread_views(spread_codes[w][rows(1)], codes[w][rows(1)])
+            nc.scalar.copy(out=dst, in_=src)
+
+        def spread_plane(w):
+            dst, src = spread_views(spread_scales[w][:], scales[w][:])
+            nc.vector.tensor_copy(out=dst, in_=src)
+
+        round_weights("w1", VEC_COLS // 4)
         quantise_operand("w1")
         interleave(rounded["x0"], raw["x0"], VEC_COLS)
+        spread_plane("w1")
+        spread_words("w1")
         quantise_operand("x0")
-        products([("z1", "w1")], "x0")
+        for g in range(G):
+            product("z1", "w1", "x0", g)
         round_weights("w2", VEC_COLS // 4)
         quantise_operand("w2")
-        products([("z2", "w2")], "x0")
+        for g in range(G):
+            product("z2", "w2", "x0", g)
         copy_z1(a0)
+        interleave(rounded["dx0"], raw["dx0"], CHUNK)
         copy_z1(b0)
-        interleave(rounded["dx0"], raw["dx0"], VEC_COLS)
-        diff(a0)
+        spread_plane("w2")
         quantise_operand("dx0")
-        products([("tz1", "w1"), ("tz2", "w2")], "dx0")
-        tanh(a0)
-        diff(b0)
-        tanh(b0)
-        interleave(rounded["x1"], raw["x1"], 0)
+        for g in range(G):
+            product("tz1", "w1", "dx0", g)
+            product("tz2", "w2", "dx0", g)
+        interleave_scalar(rounded["x1"], raw["x1"], VEC_COLS)
+        diff(a0, whole)
+        tanh(a0, whole)
+        diff(b0, whole)
+        tanh(b0, whole)
+        halve(half_gain, factors)
+        interleave_vector(rounded["x1"], raw["x1"], VEC_COLS)
         interleave(rounded["dx1"], raw["dx1"], 0)
-        up(a0)
-        down(a0)
-        up(b0)
-        mix(nc.vector, a0, first)
+        up(a0, whole)
         quantise_operand("x1")
-        products([("z1", "w1"), ("z2", "w2")], "x1")
-        down(b0)
-        finish(a0, first)
-        store_y(nc.sync, 0, first)
-        mix(nc.vector, b0, first)
-        quantise_operand("dx1")
-        products([("tz1", "w1"), ("tz2", "w2")], "dx1")
+        product("z1", "w1", "x1", 0)
+        product("z2", "w2", "x1", 0)
+        spread_product("z1", "w1", "x1")
+        down(a0, whole)
+        mix(nc.gpsimd, a0, whole)
+        halve(half_gain_b1, factors_b1)
+        up(b0, whole)
+        down(b0, whole)
         copy_z1(a1)
+        spread_words("w2")
+        spread_product("z2", "w2", "x1")
+        diff(a1, whole)
+        tanh(a1, whole)
+        quantise_operand("dx1")
+        product("tz1", "w1", "dx1", 0)
+        product("tz2", "w2", "dx1", 0)
+        spread_product("tz1", "w1", "dx1")
+        spread_product("tz2", "w2", "dx1")
         copy_z1(b1)
-        diff(a1)
-        tanh(a1)
-        finish(b0, first)
-        store_y(nc.sync, 1, first)
-        diff(b1)
-        tanh(b1)
-        interleave(y_bf[first[0]], gathered[first[0]], 0)
-        up(a1)
-        down(a1)
-        up(b1)
-        mix(nc.vector, a1, both)
-        down(b1)
-        finish(a1, second)
-        mix(nc.vector, b1, second)
-        mix(nc.vector, b1, last)
-        finish(b1, second)
-        finish(a1, last)
-        finish(b1, last)
-        planes(first)
-        for g in range(G):
-            store_y(nc.scalar, g, second)
-        interleave(y_bf[second[0]], gathered[second[0]], 0)
-        for g in range(G):
-            store_y(nc.scalar, g, last)
-        interleave(y_bf[last[0]], gathered[last[0]], last[1])
-        planes(second)
-        planes(last)
+        mix(nc.vector, b0, whole)
+        finish(a0, whole)
+        gather(a0)
+        finish(b0, whole)
+        gather(b0)
+        store_y(a0)
+        store_y(b0)
+        diff(b1, whole)
+        tanh(b1, whole)
+        interleave(y_bf[a0], gathered[a0], 0)
+        interleave(y_bf[b0], gathered[b0], 0)
+        up(a1, whole)
+        down(a1, low)
+        down(a1, high)
+        mix(nc.vector, a1, low)
+        mix(nc.vector, a1, high)
+        finish(a1, whole)
+        gather(a1)
+        store_y(a1)
+        up(b1, whole)
+        quantise_y(a0)
+        quantise_y(b0)
+        for c in range(2):
+            store_words(nc.sync, 0, c)
         for quad in range(4):
-            queue = nc.scalar if quad % 2 else nc.sync
-            queue.dma_start(
-                out=out_2[0, 4 * quad : 4 * quad + 4, :].bitcast(I32),
-                in_=y_scales[32 * quad : 32 * quad + 4, :].bitcast(I32),
-            )
+            store_scales(nc.gpsimd if quad == 3 else nc.sync, 0, quad)
+        down(b1, low)
+        down(b1, high)
+        mix(nc.vector, b1, low)
+        mix(nc.vector, b1, high)
+        finish(b1, whole)
+        y_b1 = work["y", b1][:].rearrange("p (t j) -> p t j", t=PACK)
+        for c in range(2):
+            nc.sync.dma_start(out=out_0[M : 2 * M, strip(1, c)].rearrange("(s t) n -> s t n", t=PACK), in_=y_b1[rows(c)])
+        interleave(y_bf[a1], gathered[a1], 0)
+        interleave(y_bf[b1], y_b1, MM_N)
+        quantise_y(a1)
+        quantise_y(b1)
+        for c, queue in enumerate((nc.sync, nc.scalar)):
+            store_words(queue, 1, c)
+            for quad in (2 * c, 2 * c + 1):
+                store_scales(queue, 1, quad)

@@ -90,21 +90,27 @@ def tile_rows_pl_tnsoftmaxoftwo_kernel(tc, x, w1, w2, tp, dx, og, base, out_0, o
             nc.gpsimd.tensor_scalar(out=dst[:], in0=src[:, 1, 0:PACK], scalar1=0.5, scalar2=0.0, op0=ALU.mult, op1=ALU.add)
 
         def round_weights(name, vec_pairs):
-            dst = rounded[name][:].rearrange("p (h a i) j -> p a h i j", h=HALVES, i=2)
-            src = raw[name][:].rearrange("p j (a i h) -> p a h i j", h=HALVES, i=2)
+            dst = rounded[name][:].rearrange("p (h a i) j -> p a j i h", h=HALVES, i=2)
+            src = raw[name][:].rearrange("p j (a i h) -> p a j i h", h=HALVES, i=2)
             nc.vector.tensor_copy(out=dst[:, 0:vec_pairs], in_=src[:, 0:vec_pairs])
             if vec_pairs < P // 2:
                 nc.scalar.copy(out=dst[:, vec_pairs : P // 2], in_=src[:, vec_pairs : P // 2])
 
+        def walk(dst, src, start, stop):
+            return (
+                dst[:, start:stop, :].rearrange("p (c i) j -> p c j i", i=4),
+                src[:, :, start:stop].rearrange("p j (c i) -> p c j i", i=4),
+            )
+
         def interleave_vector(dst, src, stop):
-            nc.vector.tensor_copy(out=dst[:, 0:stop, :], in_=src[:].rearrange("p j c -> p c j")[:, 0:stop, :])
+            out, in_ = walk(dst, src, 0, stop)
+            nc.vector.tensor_copy(out=out, in_=in_)
 
         def interleave_scalar(dst, src, start):
             width = src.shape[2]
             if start < width:
-                nc.scalar.activation(
-                    out=dst[:, start:width, :], in_=src[:].rearrange("p j c -> p c j")[:, start:width, :], func=ACT.Copy
-                )
+                out, in_ = walk(dst, src, start, width)
+                nc.scalar.activation(out=out, in_=in_, func=ACT.Copy)
 
         def interleave(dst, src, vec_cols):
             if vec_cols > 0:
@@ -241,10 +247,10 @@ def tile_rows_pl_tnsoftmaxoftwo_kernel(tc, x, w1, w2, tp, dx, og, base, out_0, o
             )
 
         for w in weights:
-            nc.gpsimd.memset(scales[w][:].bitcast(U32), 0)
+            nc.vector.memset(scales[w][:].bitcast(U32), 0)
         for w in weights:
-            nc.gpsimd.memset(spread_scales[w][:].bitcast(U32), 0)
-            nc.gpsimd.memset(spread_codes[w][rows(1), :], 0)
+            nc.vector.memset(spread_scales[w][:].bitcast(U32), 0)
+            nc.vector.memset(spread_codes[w][rows(1), :], 0)
 
         load_operand("w1", w1)
         load_operand("x0", x[:, :, cols(0)])
@@ -291,13 +297,13 @@ def tile_rows_pl_tnsoftmaxoftwo_kernel(tc, x, w1, w2, tp, dx, og, base, out_0, o
         for g in range(G):
             product("tz1", "w1", "dx0", g)
             product("tz2", "w2", "dx0", g)
-        interleave_scalar(rounded["x1"], raw["x1"], VEC_COLS)
+        interleave_scalar(rounded["x1"], raw["x1"], CHUNK)
         diff(a0, whole)
         tanh(a0, whole)
         diff(b0, whole)
         tanh(b0, whole)
         halve(half_gain, factors)
-        interleave_vector(rounded["x1"], raw["x1"], VEC_COLS)
+        interleave_vector(rounded["x1"], raw["x1"], CHUNK)
         interleave(rounded["dx1"], raw["dx1"], 0)
         up(a0, whole)
         quantise_operand("x1")

@@ -141,12 +141,13 @@ def tile_rows_pl_tnsoftmaxoftwo_kernel(tc, x, w1, w2, tp, dx, og, base, out_0, o
                 stop=stop,
             )
 
-        def product(result, w, moving, g):
+        def product(result, w, moving, groups):
             for h in range(HALVES):
                 m_cols = slice(h * P, (h + 1) * P)
                 for n0 in range(0, CHUNK, MM_N):
-                    out = bank[result, g][:, h * CHUNK + n0 : h * CHUNK + n0 + MM_N]
-                    matmul(out, codes[w][rows(g), m_cols], scales[w][rows(g), m_cols], moving, g, n0, True, True)
+                    for g in groups:
+                        out = bank[result, g][:, h * CHUNK + n0 : h * CHUNK + n0 + MM_N]
+                        matmul(out, codes[w][rows(g), m_cols], scales[w][rows(g), m_cols], moving, g, n0, True, True)
 
         def spread_product(result, w, moving):
             for t in range(PACK):
@@ -283,20 +284,18 @@ def tile_rows_pl_tnsoftmaxoftwo_kernel(tc, x, w1, w2, tp, dx, og, base, out_0, o
         spread_plane("w1")
         spread_words("w1")
         quantise_operand("x0")
-        for g in range(G):
-            product("z1", "w1", "x0", g)
+        product("z1", "w1", "x0", range(G))
         round_weights("w2", VEC_COLS // 4)
         quantise_operand("w2")
         for g in range(G):
-            product("z2", "w2", "x0", g)
+            product("z2", "w2", "x0", [g])
         copy_z1(a0)
         interleave(rounded["dx0"], raw["dx0"], CHUNK)
         copy_z1(b0)
         spread_plane("w2")
         quantise_operand("dx0")
-        for g in range(G):
-            product("tz1", "w1", "dx0", g)
-            product("tz2", "w2", "dx0", g)
+        product("tz1", "w1", "dx0", range(G))
+        product("tz2", "w2", "dx0", range(G))
         interleave_scalar(rounded["x1"], raw["x1"], CHUNK)
         diff(a0, whole)
         tanh(a0, whole)
@@ -307,8 +306,8 @@ def tile_rows_pl_tnsoftmaxoftwo_kernel(tc, x, w1, w2, tp, dx, og, base, out_0, o
         interleave(rounded["dx1"], raw["dx1"], 0)
         up(a0, whole)
         quantise_operand("x1")
-        product("z1", "w1", "x1", 0)
-        product("z2", "w2", "x1", 0)
+        product("z1", "w1", "x1", [0])
+        product("z2", "w2", "x1", [0])
         spread_product("z1", "w1", "x1")
         down(a0, whole)
         mix(nc.gpsimd, a0, whole)
@@ -321,8 +320,8 @@ def tile_rows_pl_tnsoftmaxoftwo_kernel(tc, x, w1, w2, tp, dx, og, base, out_0, o
         diff(a1, whole)
         tanh(a1, whole)
         quantise_operand("dx1")
-        product("tz1", "w1", "dx1", 0)
-        product("tz2", "w2", "dx1", 0)
+        product("tz1", "w1", "dx1", [0])
+        product("tz2", "w2", "dx1", [0])
         spread_product("tz1", "w1", "dx1")
         spread_product("tz2", "w2", "dx1")
         copy_z1(b1)

from contextlib import ExitStack

import concourse.mybir as mybir

G, D, M, N = 2, 256, 256, 512
FLOPS = 4 * 2 * G * D * M * N

F32 = mybir.dt.float32
BF16 = mybir.dt.bfloat16
U32 = mybir.dt.uint32
I32 = mybir.dt.int32
U8 = mybir.dt.uint8
FP8X4 = mybir.dt.float8_e4m3fn_x4
ACT = mybir.ActivationFunctionType
ALU = mybir.AluOpType

P = 128
PACK = 4
ROWS = D // PACK
HALVES = M // P
CHUNK = 256
CHUNKS = N // CHUNK
MM_N = 128
VEC_COLS = 176
BANK = HALVES * CHUNK
SPREAD = (2 * PACK + 1) * ROWS


def tile_rows_pl_tnsoftmaxoftwo_kernel(tc, x, w1, w2, tp, dx, og, base, out_0, out_1, out_2):
    nc = tc.nc
    with ExitStack() as ctx:
        sb = ctx.enter_context(tc.tile_pool(name="sb", bufs=1))
        ps = ctx.enter_context(tc.psum_pool(name="ps", bufs=1))
        ctx.enter_context(tc.manual_schedule())

        def sbuf(name, shape, dtype):
            return sb.tile(shape, dtype, name=name, align_bytes=64)

        def cols(k):
            return slice(k * CHUNK, (k + 1) * CHUNK)

        def rows(i):
            return slice(i * ROWS, (i + 1) * ROWS)

        def strip(k, c):
            return slice(k * CHUNK + c * MM_N, k * CHUNK + (c + 1) * MM_N)

        weights = ("w1", "w2")
        operands = list(weights) + [a + str(k) for a in ("x", "dx") for k in range(CHUNKS)]
        raw = {o: sbuf(o + "_raw", [P, PACK, CHUNK], F32) for o in operands}
        rounded = {o: sbuf(o + "_bf", [P, CHUNK, PACK], BF16) for o in operands}
        codes = {o: sbuf(o + "_codes", [P, CHUNK], U32) for o in operands}
        scales = {o: sbuf(o + "_scales", [P, CHUNK], U8) for o in operands}
        spread_codes = {w: sbuf(w + "_spread_codes", [P, SPREAD], U32) for w in weights}
        spread_scales = {w: sbuf(w + "_spread_scales", [P, SPREAD], U8) for w in weights}
        units = [(g, k) for k in range(CHUNKS) for g in range(G)]
        a0, b0, a1, b1 = units
        base_0 = sbuf("base_0", [P, HALVES, N], F32)
        base_b0 = sbuf("base_b0", [P, HALVES, CHUNK], F32)
        base_b1 = sbuf("base_b1", [P, PACK, MM_N], F32)
        factors = sbuf("factors", [P, 2, 8], F32)
        factors_b1 = sbuf("factors_b1", [P, 2, 8], F32)
        half_gain = sbuf("half_gain", [P, PACK], F32)
        half_gain_b1 = sbuf("half_gain_b1", [P, PACK], F32)
        work = {
            (s, u): sbuf("%s_%d%d" % (s, u[0], u[1]), [P, BANK], F32)
            for s in ("z1", "diff", "tanh", "up", "down", "mix", "y")
            for u in units
        }
        gathered = {u: sbuf("gathered_%d%d" % u, [P, PACK, MM_N], F32) for u in (a0, b0, a1)}
        y_bf = {u: sbuf("y_bf_%d%d" % u, [P, MM_N, PACK], BF16) for u in units}
        y_codes = [sbuf("y_codes%d" % k, [P, CHUNK], U32) for k in range(CHUNKS)]
        y_scales = [sbuf("y_scales%d" % k, [P, CHUNK], U8) for k in range(CHUNKS)]
        bank = {
            (s, g): ps.tile([P, BANK], F32, name="%s_bank%d" % (s, g))
            for s in ("z1", "z2", "tz1", "tz2")
            for g in range(G)
        }

        def load_operand(name, src):
            nc.sync.dma_start(out=raw[name][:], in_=src.rearrange("g (p j) c -> (g p) j c", j=PACK))

        def load_factor(queue, which, src):
            queue.dma_start(
                out=factors[:, which, 0 : G * HALVES].rearrange("q (g h) -> q g h", h=HALVES),
                in_=src.rearrange("g (q h) o -> q g (h o)", h=HALVES),
            )

        def halve(dst, src):
            nc.gpsimd.tensor_scalar(out=dst[:], in0=src[:, 1, 0:PACK], scalar1=0.5, scalar2=0.0, op0=ALU.mult, op1=ALU.add)

        def round_weights(name, vec_pairs):
            dst = rounded[name][:].rearrange("p (h a i) j -> p a j i h", h=HALVES, i=2)
            src = raw[name][:].rearrange("p j (a i h) -> p a j i h", h=HALVES, i=2)
            nc.vector.tensor_copy(out=dst[:, 0:vec_pairs], in_=src[:, 0:vec_pairs])
            if vec_pairs < P // 2:
                nc.scalar.copy(out=dst[:, vec_pairs : P // 2], in_=src[:, vec_pairs : P // 2])

        def walk(dst, src, start, stop):
            return (
                dst[:, start:stop, :].rearrange("p (c i) j -> p c j i", i=4),
                src[:, :, start:stop].rearrange("p j (c i) -> p c j i", i=4),
            )

        def interleave_vector(dst, src, stop):
            out, in_ = walk(dst, src, 0, stop)
            nc.vector.tensor_copy(out=out, in_=in_)

        def interleave_scalar(dst, src, start):
            width = src.shape[2]
            if start < width:
                out, in_ = walk(dst, src, start, width)
                nc.scalar.activation(out=out, in_=in_, func=ACT.Copy)

        def interleave(dst, src, vec_cols):
            if vec_cols > 0:
                interleave_vector(dst, src, vec_cols)
            interleave_scalar(dst, src, vec_cols)

        def quantise(words, plane, src):
            nc.vector.quantize_mx(out=words.bitcast(FP8X4), scales=plane, in_=src[:].rearrange("p c j -> p (c j)"))

        def quantise_operand(name):
            quantise(codes[name][:], scales[name][:], rounded[name])

        def spread_views(dst, src):
            return (
                dst[:, ROWS:SPREAD].rearrange("p (a h z s) -> p a h z s", a=2, h=HALVES, z=2)[:, :, :, 0, :],
                src.rearrange("p (h s a) -> p a h s", h=HALVES, a=2),
            )

        def matmul(out, w_codes, w_scales, moving, g, n0, start, stop):
            n_cols = slice(n0, n0 + MM_N)
            nc.tensor.matmul_mx(
                out=out,
                lhsT=w_codes.bitcast(FP8X4),
                lhsT_scale=w_scales,
                rhs=codes[moving][rows(g), n_cols].bitcast(FP8X4),
                rhs_scale=scales[moving][rows(g), n_cols],
                start=start,
                stop=stop,
            )

        def product(result, w, moving, groups):
            for h in range(HALVES):
                m_cols = slice(h * P, (h + 1) * P)
                for n0 in range(0, CHUNK, MM_N):
                    for g in groups:
                        out = bank[result, g][:, h * CHUNK + n0 : h * CHUNK + n0 + MM_N]
                        matmul(out, codes[w][rows(g), m_cols], scales[w][rows(g), m_cols], moving, g, n0, True, True)

        def spread_product(result, w, moving):
            for t in range(PACK):
                out = bank[result, 1][:, t * MM_N : (t + 1) * MM_N]
                for c in range(2):
                    m_cols = slice((2 * t + 1 - c) * ROWS, (2 * t + 1 - c) * ROWS + P)
                    matmul(
                        out, spread_codes[w][rows(1), m_cols], spread_scales[w][rows(1), m_cols], moving, 1, c * MM_N,
                        c == 0, c == 1,
                    )

        whole = slice(0, BANK)
        low, high = slice(0, BANK // 2), slice(BANK // 2, BANK)

        def pieces(u, part):
            if u == b1:
                return [(slice(n0, n0 + MM_N), n0 // MM_N) for n0 in range(part.start, part.stop, MM_N)]
            return [(slice(n0, n0 + CHUNK), u[0] * HALVES + n0 // CHUNK) for n0 in range(part.start, part.stop, CHUNK)]

        def copy_z1(u):
            nc.scalar.activation(out=work["z1", u][:], in_=bank["z1", u[0]][:], func=ACT.Copy, scale=0.5)

        def diff(u, part):
            nc.vector.scalar_tensor_tensor(
                out=work["diff", u][:, part], in0=bank["z2", u[0]][:, part], scalar=-0.5, in1=work["z1", u][:, part],
                op0=ALU.mult, op1=ALU.add,
            )

        def tanh(u, part):
            temper = factors_b1 if u == b1 else factors
            for piece, i in pieces(u, part):
                nc.scalar.activation(
                    out=work["tanh", u][:, piece], in_=work["diff", u][:, piece], func=ACT.Tanh, scale=temper[:, 0, i : i + 1]
                )

        def up(u, part):
            nc.vector.scalar_tensor_tensor(
                out=work["up", u][:, part], in0=work["tanh", u][:, part], scalar=1.0, in1=bank["tz1", u[0]][:, part],
                op0=ALU.add, op1=ALU.mult,
            )

        def down(u, part):
            nc.vector.scalar_tensor_tensor(
                out=work["down", u][:, part], in0=work["tanh", u][:, part], scalar=1.0, in1=bank["tz2", u[0]][:, part],
                op0=ALU.subtract, op1=ALU.mult,
            )

        def mix(engine, u, part):
            engine.tensor_tensor(
                out=work["mix", u][:, part], in0=work["up", u][:, part], in1=work["down", u][:, part], op=ALU.subtract
            )

        def base_of(u, i):
            if u == b1:
                return base_b1[:, i, :]
            if u == b0:
                return base_b0[:, i - HALVES, :]
            return base_0[:, i, cols(u[1])]

        def finish(u, part):
            gain = half_gain_b1 if u == b1 else half_gain
            for piece, i in pieces(u, part):
                nc.vector.scalar_tensor_tensor(
                    out=work["y", u][:, piece], in0=work["mix", u][:, piece], scalar=gain[:, i : i + 1], in1=base_of(u, i),
                    op0=ALU.mult, op1=ALU.add,
                )

        def store_y(u):
            g, k = u
            nc.sync.dma_start(
                out=out_0[g * M : (g + 1) * M, cols(k)].rearrange("(q h) c -> q h c", h=HALVES),
                in_=work["y", u][:].rearrange("q (h c) -> q h c", h=HALVES),
            )

        def gather(u):
            y = work["y", u][:].rearrange("q (h c) -> q h c", h=HALVES)
            for c in range(2):
                nc.sync.dma_start(out=gathered[u][rows(c)], in_=y[:, :, c * MM_N : (c + 1) * MM_N])

        def quantise_y(u):
            g, k = u
            window = slice(g * MM_N, (g + 1) * MM_N)
            quantise(y_codes[k][:, window], y_scales[k][:, window], y_bf[u])

        words_out = out_1.rearrange("s p n u -> (s p) (n u)").bitcast(I32)

        def store_words(queue, k, c):
            queue.dma_start(
                out=words_out[:, strip(k, c)].rearrange("(g s) j -> s g j", g=G),
                in_=y_codes[k][rows(c), :].bitcast(I32).rearrange("s (g j) -> s g j", g=G),
            )

        def store_scales(queue, k, quad):
            first_row = 4 * (quad % 2)
            queue.dma_start(
                out=out_2[0, :, strip(k, quad // 2)].bitcast(I32).rearrange("(g f) j -> f g j", g=G)[first_row : first_row + 4],
                in_=y_scales[k][32 * quad : 32 * quad + 4, :].bitcast(I32).rearrange("r (g j) -> r g j", g=G),
            )

        for w in weights:
            nc.vector.memset(scales[w][:].bitcast(U32), 0)
        for w in weights:
            nc.vector.memset(spread_scales[w][:].bitcast(U32), 0)
            nc.vector.memset(spread_codes[w][rows(1), :], 0)

        load_operand("w1", w1)
        load_operand("x0", x[:, :, cols(0)])
        load_operand("w2", w2)
        load_operand("dx0", dx[:, :, cols(0)])
        load_factor(nc.sync, 0, tp)
        load_operand("x1", x[:, :, cols(1)])
        load_operand("dx1", dx[:, :, cols(1)])
        load_factor(nc.sync, 1, og)
        nc.sync.dma_start(out=base_0[:], in_=base[0].rearrange("(q h) n -> q h n", h=HALVES))
        nc.sync.dma_start(out=base_b0[:], in_=base[1, :, cols(0)].rearrange("(q h) n -> q h n", h=HALVES))
        for c in range(2):
            for which, src in enumerate((tp, og)):
                nc.sync.dma_start(
                    out=factors_b1[rows(c), which, 0:PACK], in_=src[1].rearrange("(s t) o -> s (t o)", t=PACK)
                )
            nc.sync.dma_start(out=base_b1[rows(c)], in_=base[1, :, strip(1, c)].rearrange("(s t) n -> s t n", t=PACK))

        def spread_words(w):
            dst, src = spread_views(spread_codes[w][rows(1)], codes[w][rows(1)])
            nc.scalar.copy(out=dst, in_=src)

        def spread_plane(w):
            dst, src = spread_views(spread_scales[w][:], scales[w][:])
            nc.vector.tensor_copy(out=dst, in_=src)

        round_weights("w1", VEC_COLS // 4)
        quantise_operand("w1")
        interleave(rounded["x0"], raw["x0"], VEC_COLS)
        spread_plane("w1")
        spread_words("w1")
        quantise_operand("x0")
        product("z1", "w1", "x0", range(G))
        round_weights("w2", VEC_COLS // 4)
        quantise_operand("w2")
        for g in range(G):
            product("z2", "w2", "x0", [g])
        copy_z1(a0)
        interleave(rounded["dx0"], raw["dx0"], CHUNK)
        copy_z1(b0)
        spread_plane("w2")
        quantise_operand("dx0")
        product("tz1", "w1", "dx0", range(G))
        product("tz2", "w2", "dx0", range(G))
        interleave_scalar(rounded["x1"], raw["x1"], CHUNK)
        diff(a0, whole)
        tanh(a0, whole)
        diff(b0, whole)
        tanh(b0, whole)
        halve(half_gain, factors)
        interleave_vector(rounded["x1"], raw["x1"], CHUNK)
        interleave(rounded["dx1"], raw["dx1"], 0)
        up(a0, whole)
        quantise_operand("x1")
        product("z1", "w1", "x1", [0])
        product("z2", "w2", "x1", [0])
        spread_product("z1", "w1", "x1")
        down(a0, whole)
        mix(nc.gpsimd, a0, whole)
        halve(half_gain_b1, factors_b1)
        up(b0, whole)
        down(b0, whole)
        copy_z1(a1)
        spread_words("w2")
        spread_product("z2", "w2", "x1")
        diff(a1, whole)
        tanh(a1, whole)
        quantise_operand("dx1")
        product("tz1", "w1", "dx1", [0])
        product("tz2", "w2", "dx1", [0])
        spread_product("tz1", "w1", "dx1")
        spread_product("tz2", "w2", "dx1")
        copy_z1(b1)
        mix(nc.vector, b0, whole)
        finish(a0, whole)
        gather(a0)
        finish(b0, whole)
        gather(b0)
        store_y(a0)
        store_y(b0)
        diff(b1, whole)
        tanh(b1, whole)
        interleave(y_bf[a0], gathered[a0], 0)
        interleave(y_bf[b0], gathered[b0], 0)
        up(a1, whole)
        down(a1, low)
        down(a1, high)
        mix(nc.vector, a1, low)
        mix(nc.vector, a1, high)
        finish(a1, whole)
        gather(a1)
        store_y(a1)
        up(b1, whole)
        quantise_y(a0)
        quantise_y(b0)
        for c in range(2):
            store_words(nc.sync, 0, c)
        for quad in range(4):
            store_scales(nc.gpsimd if quad == 3 else nc.sync, 0, quad)
        down(b1, low)
        down(b1, high)
        mix(nc.vector, b1, low)
        mix(nc.vector, b1, high)
        finish(b1, whole)
        y_b1 = work["y", b1][:].rearrange("p (t j) -> p t j", t=PACK)
        for c in range(2):
            nc.sync.dma_start(out=out_0[M : 2 * M, strip(1, c)].rearrange("(s t) n -> s t n", t=PACK), in_=y_b1[rows(c)])
        interleave(y_bf[a1], gathered[a1], 0)
        interleave(y_bf[b1], y_b1, MM_N)
        quantise_y(a1)
        quantise_y(b1)
        for c, queue in enumerate((nc.sync, nc.scalar)):
            store_words(queue, 1, c)
            for quad in (2 * c, 2 * c + 1):
                store_scales(queue, 1, quad)
